import numpy as np
import ml_dtypes


def mxq(x, axis, fmt="e4m3"):
    dtype, down = {"e4m3": (ml_dtypes.float8_e4m3fn, 7), "e5m2": (ml_dtypes.float8_e5m2, 14)}[fmt]
    v = np.moveaxis(np.asarray(x, np.float32).astype(ml_dtypes.bfloat16).astype(np.float64), axis, -1)
    blocks = v.reshape(v.shape[:-1] + (-1, 32))
    amax = np.abs(blocks).max(-1, keepdims=True)
    byte = np.maximum(np.where(amax > 0, np.frexp(amax)[1] - 1 + 127, 0) - down, 1)
    scale = np.exp2(byte - 127.0)
    codes = (blocks / scale).astype(np.float32).astype(dtype).astype(np.float64)
    return np.moveaxis((codes * scale).reshape(v.shape), -1, axis)


WIDE = False


def mx_kscale(k):
    if not WIDE:
        return np.ones(k)
    levels = np.array([30, -30])
    if k % 512:
        return np.exp2(np.random.permutation(np.resize(levels, k // 32))).repeat(32)
    a = np.empty((k // 512, 16))
    for p in range(k // 512):
        a[p, :8] = np.random.permutation(np.resize(levels, 8))
        for g in range(8):
            far = levels[np.abs(levels - a[p, g]) >= 10]
            a[p, g + 8] = far[np.random.randint(len(far))]
    return np.exp2(a.ravel()).repeat(32)


def f64(x):
    return np.asarray(x).astype(np.float64)


E2M1 = np.array([0.0, 0.5, 1.0, 1.5, 2.0, 3.0, 4.0, 6.0, -0.0, -0.5, -1.0, -1.5, -2.0, -3.0, -4.0, -6.0])


def pack_weight(w, fmt):
    k, n = w.shape
    w = f64(np.asarray(w, np.float32).astype(ml_dtypes.bfloat16)).reshape(k // 32, 32, n)
    amax = np.abs(w).max(1)
    if fmt == "e4m3":
        byte = np.frexp(amax)[1] - 1 + 127 - 7
    else:
        mant, ex = np.frexp(amax / 6.0)
        byte = np.where(mant > 0.5, ex, ex - 1) + 127
    byte = np.clip(np.where(amax > 0, byte, 1), 1, 254)
    scaled = (w * np.exp2(127.0 - byte)[:, None, :]).reshape(k, n).astype(np.float32)
    by_word = np.ascontiguousarray(scaled.reshape(k // 512, 128, 4, n).transpose(0, 1, 3, 2))
    if fmt == "e4m3":
        words = by_word.astype(ml_dtypes.float8_e4m3fn).view(np.uint8)
    else:
        c = by_word.astype(ml_dtypes.float4_e2m1fn).view(np.uint8) & 0xF
        words = (c[..., 0::2] | (c[..., 1::2] << 4)).reshape(k // 512, 128, 2 * n)
    return np.ascontiguousarray(words), np.ascontiguousarray(byte.astype(np.uint8).reshape(k // 512, 16, n))


def unpack_weight(words, scales, fmt):
    g, _, n = scales.shape
    words = np.ascontiguousarray(words).reshape(g, 128, n, -1)
    if fmt == "e4m3":
        vals = words.view(ml_dtypes.float8_e4m3fn).astype(np.float64)
    else:
        nib = np.empty((g, 128, n, 4), np.uint8)
        nib[..., 0::2] = words & 0xF
        nib[..., 1::2] = words >> 4
        vals = E2M1[nib]
    vals = vals * np.repeat(np.exp2(scales.astype(np.float64) - 127.0), 8, axis=1)[..., None]
    return vals.transpose(0, 1, 3, 2).reshape(g * 512, n)


def planes(y):
    n, m = y.shape
    v = y.astype(np.float32).astype(ml_dtypes.bfloat16).astype(np.float64).reshape(n // 32, 32, m)
    top = np.abs(v).max(1)
    byte = np.clip(np.where(top > 0, np.frexp(top)[1] - 1 + 127 - 7, 1), 1, 254)
    codes = (v * np.exp2(127.0 - byte)[:, None, :]).reshape(n, m).astype(np.float32).astype(ml_dtypes.float8_e4m3fn).view(np.uint8)
    words = codes.reshape(n // 512, 128, 4, m).transpose(0, 1, 3, 2)
    return np.ascontiguousarray(words), np.ascontiguousarray(byte.astype(np.uint8).reshape(n // 512, 16, m))


K, L, R, M, T = 512, 1024, 512, 1536, 1024


def setup_inputs():
    n = np.random.standard_normal
    s1 = mx_kscale(K)[:, None]
    s2 = mx_kscale(L)[:, None]
    u = mx_kscale(R)[:, None]
    p_w = pack_weight(n((R, M)) / np.sqrt(R) / u, "e2m1")
    return {
        "x": (n((K, T)) * s1).astype(np.float32),
        "wx": (n((K, R)) / np.sqrt(K) / s1 * u.T).astype(np.float32),
        "c": (n((L, T)) * s2).astype(np.float32),
        "wc": (n((L, R)) / np.sqrt(L) / s2).astype(np.float32),
        "w_words": p_w[0],
        "w_scales": p_w[1],
        "g": (n((1024, 1536))).astype(np.float32),
    }


def reference(x, wx, c, wc, w_words, w_scales, g):
    x_ = mxq(f64(x), 0, "e4m3")
    wx_ = mxq(f64(wx), 0, "e4m3")
    c_ = mxq(f64(c), 0, "e5m2")
    wc_ = mxq(f64(wc), 0, "e4m3")
    w_ = unpack_weight(w_words, w_scales, "e2m1")
    h_ = mxq((wx_.T @ x_) * (wc_.T @ c_), 0, "e4m3")
    y = h_.T @ w_
    out_0 = f64(g) * y
    return (out_0,) + planes(out_0)

@@ -1,0 +1,249 @@
+from contextlib import ExitStack
+
+import concourse.mybir as mybir
+
+K, L, R, M, T = 512, 1024, 512, 1536, 1024
+FLOPS = 2 * (K * R * T + L * R * T + R * T * M)
+
+F32 = mybir.dt.float32
+BF16 = mybir.dt.bfloat16
+I32 = mybir.dt.int32
+U32 = mybir.dt.uint32
+U8 = mybir.dt.uint8
+E4M3 = mybir.dt.float8_e4m3fn_x4
+E5M2 = mybir.dt.float8_e5m2_x4
+E2M1 = mybir.dt.float4_e2m1fn_x4
+MULT = mybir.AluOpType.mult
+
+P = 128
+PACK = 4
+PASS = P * PACK
+BANK = 512
+HALVES = T // PASS
+CHUNKS = M // BANK
+QUADRANTS = 4
+
+
+def tile_mix_bilin_tm_pl_mul_kernel(tc, x, wx, c, wc, w_words, w_scales, g, out_0, out_1, out_2):
+    nc = tc.nc
+
+    with ExitStack() as ctx:
+        keep = ctx.enter_context(tc.tile_pool(name="keep", bufs=1))
+        stage = ctx.enter_context(tc.tile_pool(name="stage", bufs=8))
+        psum = ctx.enter_context(tc.psum_pool(name="psum", bufs=8))
+        ctx.enter_context(tc.manual_schedule())
+
+        def load_pass(name, rows):
+            raw = keep.tile([P, PACK * BANK], F32, name=name)
+            nc.sync.dma_start(
+                out=raw[:].rearrange("p (j w) -> p j w", j=PACK),
+                in_=rows.rearrange("(p j) w -> p j w", j=PACK),
+            )
+            return raw
+
+        def copy_on(engine, out, in_):
+            if engine == "scalar":
+                nc.scalar.copy(out=out, in_=in_)
+            else:
+                nc.vector.tensor_copy(out=out, in_=in_)
+
+        def round_plain(engine, rows):
+            rounded = stage.tile([P, PACK * BANK], BF16, tag="rounded", align_bytes=64)
+            copy_on(
+                engine,
+                rounded[:].rearrange("p (c u j) -> p c j u", u=4, j=PACK),
+                rows.rearrange("p j (c u) -> p c j u", u=4),
+            )
+            return rounded
+
+        def round_dealt(engine, raw):
+            rounded = stage.tile([P, PACK * BANK], BF16, tag="rounded", align_bytes=64)
+            copy_on(
+                engine,
+                rounded[:].rearrange("p (i m j) -> p m j i", i=PACK, j=PACK),
+                raw[:].rearrange("p (j m i) -> p m j i", i=PACK, j=PACK),
+            )
+            return rounded
+
+        def quantize(name, rounded, fmt):
+            codes = keep.tile([P, BANK], U32, name=name + "_codes", align_bytes=64)
+            scales = keep.tile([P, BANK], U8, name=name + "_scales", align_bytes=64)
+            nc.vector.quantize_mx(out=codes[:].bitcast(fmt), scales=scales[:], in_=rounded[:])
+            return codes, scales
+
+        def rows_of(raw):
+            return raw[:].rearrange("p (j w) -> p j w", j=PACK)
+
+        def tokens(a):
+            return slice(a * PASS, (a + 1) * PASS)
+
+        w_plane = keep.tile([P, M], U8, align_bytes=64)
+        nc.vector.memset(w_plane[:].bitcast(I32), 0)
+
+        wc_raw, c_raw, x_raw = {}, {}, {}
+        for s in range(2):
+            wc_raw[s] = load_pass("wc_raw%d" % s, wc[s * PASS : (s + 1) * PASS, :])
+            c_raw[0, s] = load_pass("c_raw0%d" % s, c[s * PASS : (s + 1) * PASS, tokens(0)])
+        for q in range(QUADRANTS):
+            nc.scalar.dma_start(
+                out=w_plane[32 * q : 32 * q + 4, :].bitcast(I32),
+                in_=w_scales[0, 4 * q : 4 * q + 4, :].bitcast(I32),
+            )
+        wx_raw = load_pass("wx_raw", wx)
+        x_raw[0] = load_pass("x_raw0", x[:, tokens(0)])
+        w_codes = keep.tile([P, 2 * M], U8, align_bytes=64)
+        nc.sync.dma_start(out=w_codes[:].bitcast(I32), in_=w_words[0].bitcast(I32))
+        for s in range(2):
+            c_raw[1, s] = load_pass("c_raw1%d" % s, c[s * PASS : (s + 1) * PASS, tokens(1)])
+        x_raw[1] = load_pass("x_raw1", x[:, tokens(1)])
+        gated = {}
+        for a in range(HALVES):
+            gated[a] = keep.tile([P, PACK, M], F32, name="gated%d" % a)
+            g_rows = g[tokens(a), :].rearrange("(p i) n -> p i n", i=PACK)
+            for pair in range(2):
+                pair_rows = slice(2 * pair, 2 * (pair + 1))
+                nc.sync.dma_start(out=gated[a][:, pair_rows, :], in_=g_rows[:, pair_rows, :])
+
+        def project_c(a, wc_q, c_q):
+            pc = keep.tile([P, PACK * BANK], F32, name="pc%d" % a)
+            for j in range(PACK):
+                bank = psum.tile([P, BANK], F32, tag="bank")
+                cols = slice(j * P, (j + 1) * P)
+                for s in range(2):
+                    nc.tensor.matmul_mx(
+                        out=bank[:],
+                        lhsT=wc_q[s][0][:, cols].bitcast(E4M3),
+                        lhsT_scale=wc_q[s][1][:, cols],
+                        rhs=c_q[s][0][:].bitcast(E5M2),
+                        rhs_scale=c_q[s][1][:],
+                        start=(s == 0),
+                        stop=(s == 1),
+                    )
+                nc.scalar.copy(
+                    out=pc[:, j * BANK : (j + 1) * BANK].rearrange("p (i m) -> p i m", i=PACK),
+                    in_=bank[:].rearrange("p (m i) -> p i m", i=PACK),
+                )
+            return pc
+
+        def project_x_and_pool(wx_q, x_q, pc):
+            rounded = stage.tile([P, PACK * BANK], BF16, tag="rounded", align_bytes=64)
+            pc_view = pc[:].rearrange("p (j i c u) -> p i c j u", j=PACK, i=PACK, u=4)
+            for i in range(PACK):
+                bank = psum.tile([P, BANK], F32, tag="bank")
+                t_cols = slice(i * P, (i + 1) * P)
+                for j in range(PACK):
+                    cols = slice(j * P, (j + 1) * P)
+                    nc.tensor.matmul_mx(
+                        out=bank[:, cols],
+                        lhsT=wx_q[0][:, cols].bitcast(E4M3),
+                        lhsT_scale=wx_q[1][:, cols],
+                        rhs=x_q[0][:, t_cols].bitcast(E4M3),
+                        rhs_scale=x_q[1][:, t_cols],
+                        start=True,
+                        stop=True,
+                    )
+                nc.vector.tensor_tensor(
+                    out=rounded[:, i * BANK : (i + 1) * BANK].rearrange("p (c u j) -> p c j u", u=4, j=PACK),
+                    in0=bank[:].rearrange("p (j c u) -> p c j u", j=PACK, u=4),
+                    in1=pc_view[:, i],
+                    op=MULT,
+                )
+            return rounded
+
+        def gate(a, h_q, i, n):
+            bank = psum.tile([P, BANK], F32, tag="bank")
+            cols = slice(i * P, (i + 1) * P)
+            nc.tensor.matmul_mx(
+                out=bank[:],
+                lhsT=h_q[0][:, cols].bitcast(E4M3),
+                lhsT_scale=h_q[1][:, cols],
+                rhs=w_codes[:, 2 * n * BANK : 2 * (n + 1) * BANK].bitcast(E2M1),
+                rhs_scale=w_plane[:, n * BANK : (n + 1) * BANK],
+                start=True,
+                stop=True,
+            )
+            part = gated[a][:, i, n * BANK : (n + 1) * BANK]
+            nc.vector.tensor_tensor(out=part, in0=bank[:], in1=part, op=MULT)
+
+        out_codes = {}
+        for a in range(HALVES):
+            out_codes[a] = keep.tile([P, M], U32, name="out_codes%d" % a, align_bytes=64)
+        out_scales = keep.tile([P, HALVES * M], U8, align_bytes=64)
+
+        def round_out(engine, a, n):
+            rounded = stage.tile([P, PACK * BANK], BF16, tag="rounded", align_bytes=64)
+            copy_on(
+                engine,
+                rounded[:].rearrange("p (n i) -> p n i", i=PACK),
+                gated[a][:, :, n * BANK : (n + 1) * BANK].rearrange("p i n -> p n i"),
+            )
+            return rounded
+
+        def quantize_out(a, n, rounded):
+            nc.vector.quantize_mx(
+                out=out_codes[a][:, n * BANK : (n + 1) * BANK].bitcast(E4M3),
+                scales=out_scales[:, a * M + n * BANK : a * M + (n + 1) * BANK],
+                in_=rounded[:],
+            )
+
+        def store_pair(a, pair):
+            pair_rows = slice(2 * pair, 2 * (pair + 1))
+            out_rows = out_0[tokens(a), :].rearrange("(p i) n -> p i n", i=PACK)
+            nc.sync.dma_start(out=out_rows[:, pair_rows, :], in_=gated[a][:, pair_rows, :])
+
+        def store_codes(a):
+            nc.sync.dma_start(
+                out=out_1[a].rearrange("p n i -> p (n i)").bitcast(I32),
+                in_=out_codes[a][:].bitcast(I32),
+            )
+
+        wc_q, c_q = {}, {}
+        for s in range(2):
+            wc_rounded = round_dealt("scalar", wc_raw[s])
+            c_rounded = round_plain("vector", rows_of(c_raw[0, s]))
+            wc_q[s] = quantize("wc%d" % s, wc_rounded, E4M3)
+            c_q[s] = quantize("c0%d" % s, c_rounded, E5M2)
+        pc = project_c(0, wc_q, c_q)
+        wx_q = quantize("wx", round_dealt("vector", wx_raw), E4M3)
+        x_q = quantize("x0", round_dealt("vector", x_raw[0]), E4M3)
+        h_q = {0: quantize("h0", project_x_and_pool(wx_q, x_q, pc), E4M3)}
+
+        c_q[0] = quantize("c10", round_plain("scalar", rows_of(c_raw[1, 0])), E5M2)
+        c_rounded = round_plain("scalar", rows_of(c_raw[1, 1]))
+        x_rounded = round_dealt("vector", x_raw[1])
+        c_q[1] = quantize("c11", c_rounded, E5M2)
+        x_q = quantize("x1", x_rounded, E4M3)
+        pc = project_c(1, wc_q, c_q)
+        h_q[1] = quantize("h1", project_x_and_pool(wx_q, x_q, pc), E4M3)
+
+        out_rounded = {}
+        for i in range(2):
+            for n in range(CHUNKS):
+                gate(0, h_q[0], i, n)
+        store_pair(0, 0)
+        for n in range(CHUNKS):
+            for i in range(2, PACK):
+                gate(0, h_q[0], i, n)
+            out_rounded[0, n] = round_out("scalar", 0, n)
+        store_pair(0, 1)
+        for i in range(2):
+            for n in range(CHUNKS):
+                gate(1, h_q[1], i, n)
+            quantize_out(0, i, out_rounded[0, i])
+        store_pair(1, 0)
+        for n in range(CHUNKS):
+            for i in range(2, PACK):
+                gate(1, h_q[1], i, n)
+            if n == 0:
+                quantize_out(0, 2, out_rounded[0, 2])
+                store_codes(0)
+            out_rounded[1, n] = round_out("vector" if n == CHUNKS - 1 else "scalar", 1, n)
+        store_pair(1, 1)
+        for n in range(CHUNKS):
+            quantize_out(1, n, out_rounded[1, n])
+        store_codes(1)
+        for q in range(QUADRANTS):
+            nc.scalar.dma_start(
+                out=out_2[:, 4 * q : 4 * q + 4, :].rearrange("a r n -> r a n").bitcast(I32),
+                in_=out_scales[32 * q : 32 * q + 4, :].bitcast(I32).rearrange("r (a n) -> r a n", a=HALVES),
+            )

@@ -34,7 +34,7 @@ def tile_mix_bilin_tm_pl_mul_kernel(tc, x, wx, c, wc, w_words, w_scales, g, out_
         ctx.enter_context(tc.manual_schedule())
 
         def load_pass(name, rows):
-            raw = keep.tile([P, PACK * BANK], F32, name=name)
+            raw = keep.tile([P, PACK * rows.shape[1]], F32, name=name)
             nc.sync.dma_start(
                 out=raw[:].rearrange("p (j w) -> p j w", j=PACK),
                 in_=rows.rearrange("(p j) w -> p j w", j=PACK),
@@ -60,8 +60,8 @@ def tile_mix_bilin_tm_pl_mul_kernel(tc, x, wx, c, wc, w_words, w_scales, g, out_
             rounded = stage.tile([P, PACK * BANK], BF16, tag="rounded", align_bytes=64)
             copy_on(
                 engine,
-                rounded[:].rearrange("p (i m j) -> p m j i", i=PACK, j=PACK),
-                raw[:].rearrange("p (j m i) -> p m j i", i=PACK, j=PACK),
+                rounded[:].rearrange("p (v e m j) -> p v m j e", v=2, e=2, j=PACK),
+                raw[:].rearrange("p (j m v e) -> p v m j e", v=2, e=2, j=PACK),
             )
             return rounded
 
@@ -104,30 +104,39 @@ def tile_mix_bilin_tm_pl_mul_kernel(tc, x, wx, c, wc, w_words, w_scales, g, out_
                 pair_rows = slice(2 * pair, 2 * (pair + 1))
                 nc.sync.dma_start(out=gated[a][:, pair_rows, :], in_=g_rows[:, pair_rows, :])
 
-        def project_c(a, wc_q, c_q):
-            pc = keep.tile([P, PACK * BANK], F32, name="pc%d" % a)
+        def c_pass(bank, j, wc_pass, c_pass_q, first):
+            cols = slice(j * P, (j + 1) * P)
+            nc.tensor.matmul_mx(
+                out=bank[:],
+                lhsT=wc_pass[0][:, cols].bitcast(E4M3),
+                lhsT_scale=wc_pass[1][:, cols],
+                rhs=c_pass_q[0][:].bitcast(E5M2),
+                rhs_scale=c_pass_q[1][:],
+                start=first,
+                stop=not first,
+            )
+
+        def open_pc(wc_pass, c_pass_q):
+            banks = []
             for j in range(PACK):
                 bank = psum.tile([P, BANK], F32, tag="bank")
-                cols = slice(j * P, (j + 1) * P)
-                for s in range(2):
-                    nc.tensor.matmul_mx(
-                        out=bank[:],
-                        lhsT=wc_q[s][0][:, cols].bitcast(E4M3),
-                        lhsT_scale=wc_q[s][1][:, cols],
-                        rhs=c_q[s][0][:].bitcast(E5M2),
-                        rhs_scale=c_q[s][1][:],
-                        start=(s == 0),
-                        stop=(s == 1),
-                    )
+                c_pass(bank, j, wc_pass, c_pass_q, True)
+                banks.append(bank)
+            return banks
+
+        def close_pc(a, banks, wc_pass, c_pass_q):
+            pc = keep.tile([P, PACK * BANK], F32, name="pc%d" % a)
+            for j in range(PACK):
+                c_pass(banks[j], j, wc_pass, c_pass_q, False)
                 nc.scalar.copy(
                     out=pc[:, j * BANK : (j + 1) * BANK].rearrange("p (i m) -> p i m", i=PACK),
-                    in_=bank[:].rearrange("p (m i) -> p i m", i=PACK),
+                    in_=banks[j][:].rearrange("p (m i) -> p i m", i=PACK),
                 )
             return pc
 
         def project_x_and_pool(wx_q, x_q, pc):
             rounded = stage.tile([P, PACK * BANK], BF16, tag="rounded", align_bytes=64)
-            pc_view = pc[:].rearrange("p (j i c u) -> p i c j u", j=PACK, i=PACK, u=4)
+            pc_view = pc[:].rearrange("p (j i c u) -> p i c j u", j=PACK, i=PACK, u=2)
             for i in range(PACK):
                 bank = psum.tile([P, BANK], F32, tag="bank")
                 t_cols = slice(i * P, (i + 1) * P)
@@ -143,14 +152,14 @@ def tile_mix_bilin_tm_pl_mul_kernel(tc, x, wx, c, wc, w_words, w_scales, g, out_
                         stop=True,
                     )
                 nc.vector.tensor_tensor(
-                    out=rounded[:, i * BANK : (i + 1) * BANK].rearrange("p (c u j) -> p c j u", u=4, j=PACK),
-                    in0=bank[:].rearrange("p (j c u) -> p c j u", j=PACK, u=4),
+                    out=rounded[:, i * BANK : (i + 1) * BANK].rearrange("p (c u j) -> p c j u", u=2, j=PACK),
+                    in0=bank[:].rearrange("p (j c u) -> p c j u", j=PACK, u=2),
                     in1=pc_view[:, i],
                     op=MULT,
                 )
             return rounded
 
-        def gate(a, h_q, i, n):
+        def project_h(h_q, i, n):
             bank = psum.tile([P, BANK], F32, tag="bank")
             cols = slice(i * P, (i + 1) * P)
             nc.tensor.matmul_mx(
@@ -162,8 +171,19 @@ def tile_mix_bilin_tm_pl_mul_kernel(tc, x, wx, c, wc, w_words, w_scales, g, out_
                 start=True,
                 stop=True,
             )
+            return bank
+
+        def gate(a, h_q, i, n):
+            bank = project_h(h_q, i, n)
             part = gated[a][:, i, n * BANK : (n + 1) * BANK]
             nc.vector.tensor_tensor(out=part, in0=bank[:], in1=part, op=MULT)
+
+        def gate_on_gpsimd(a, h_q, i, n):
+            bank = project_h(h_q, i, n)
+            y_part = stage.tile([P, BANK], F32, tag="y_part", bufs=4)
+            nc.scalar.copy(out=y_part[:], in_=bank[:])
+            part = gated[a][:, i, n * BANK : (n + 1) * BANK]
+            nc.gpsimd.tensor_tensor(out=part, in0=y_part[:], in1=part, op=MULT)
 
         out_codes = {}
         for a in range(HALVES):
@@ -191,57 +211,67 @@ def tile_mix_bilin_tm_pl_mul_kernel(tc, x, wx, c, wc, w_words, w_scales, g, out_
             out_rows = out_0[tokens(a), :].rearrange("(p i) n -> p i n", i=PACK)
             nc.sync.dma_start(out=out_rows[:, pair_rows, :], in_=gated[a][:, pair_rows, :])
 
-        def store_codes(a):
+        def store_codes(a, cols):
             nc.sync.dma_start(
-                out=out_1[a].rearrange("p n i -> p (n i)").bitcast(I32),
-                in_=out_codes[a][:].bitcast(I32),
+                out=out_1[a].rearrange("p n i -> p (n i)").bitcast(I32)[:, cols],
+                in_=out_codes[a][:, cols].bitcast(I32),
             )
 
-        wc_q, c_q = {}, {}
+        wc_q = {}
         for s in range(2):
             wc_rounded = round_dealt("scalar", wc_raw[s])
             c_rounded = round_plain("vector", rows_of(c_raw[0, s]))
             wc_q[s] = quantize("wc%d" % s, wc_rounded, E4M3)
-            c_q[s] = quantize("c0%d" % s, c_rounded, E5M2)
-        pc = project_c(0, wc_q, c_q)
+            c_q = quantize("c0%d" % s, c_rounded, E5M2)
+            if s == 0:
+                pc_banks = open_pc(wc_q[0], c_q)
+        pc = close_pc(0, pc_banks, wc_q[1], c_q)
         wx_q = quantize("wx", round_dealt("vector", wx_raw), E4M3)
         x_q = quantize("x0", round_dealt("vector", x_raw[0]), E4M3)
-        h_q = {0: quantize("h0", project_x_and_pool(wx_q, x_q, pc), E4M3)}
-
-        c_q[0] = quantize("c10", round_plain("scalar", rows_of(c_raw[1, 0])), E5M2)
-        c_rounded = round_plain("scalar", rows_of(c_raw[1, 1]))
-        x_rounded = round_dealt("vector", x_raw[1])
-        c_q[1] = quantize("c11", c_rounded, E5M2)
-        x_q = quantize("x1", x_rounded, E4M3)
-        pc = project_c(1, wc_q, c_q)
-        h_q[1] = quantize("h1", project_x_and_pool(wx_q, x_q, pc), E4M3)
+        c_rounded = round_plain("scalar", rows_of(c_raw[1, 0]))
+        h_q = quantize("h0", project_x_and_pool(wx_q, x_q, pc), E4M3)
 
         out_rounded = {}
+        for n in range(CHUNKS - 1):
+            for i in range(2):
+                gate_on_gpsimd(0, h_q, i, n)
+        c_q = quantize("c10", c_rounded, E5M2)
+        pc_banks = open_pc(wc_q[0], c_q)
+        c_rounded = round_plain("vector", rows_of(c_raw[1, 1]))
+        x_rounded = round_dealt("vector", x_raw[1])
+        c_q = quantize("c11", c_rounded, E5M2)
+        x_q = quantize("x1", x_rounded, E4M3)
+        pc = close_pc(1, pc_banks, wc_q[1], c_q)
+        h_rounded = project_x_and_pool(wx_q, x_q, pc)
         for i in range(2):
-            for n in range(CHUNKS):
-                gate(0, h_q[0], i, n)
+            gate(0, h_q, i, CHUNKS - 1)
         store_pair(0, 0)
         for n in range(CHUNKS):
             for i in range(2, PACK):
-                gate(0, h_q[0], i, n)
+                gate(0, h_q, i, n)
             out_rounded[0, n] = round_out("scalar", 0, n)
+            if n == 1:
+                h_next = quantize("h1", h_rounded, E4M3)
         store_pair(0, 1)
+
+        h_q = h_next
         for i in range(2):
             for n in range(CHUNKS):
-                gate(1, h_q[1], i, n)
+                gate(1, h_q, i, n)
             quantize_out(0, i, out_rounded[0, i])
+        quantize_out(0, 2, out_rounded[0, 2])
+        store_codes(0, slice(0, M))
         store_pair(1, 0)
-        for n in range(CHUNKS):
+        for n in (0, 2, 1):
             for i in range(2, PACK):
-                gate(1, h_q[1], i, n)
-            if n == 0:
-                quantize_out(0, 2, out_rounded[0, 2])
-                store_codes(0)
-            out_rounded[1, n] = round_out("vector" if n == CHUNKS - 1 else "scalar", 1, n)
+                gate(1, h_q, i, n)
+            out_rounded[1, n] = round_out("vector" if n == 1 else "scalar", 1, n)
         store_pair(1, 1)
         for n in range(CHUNKS):
             quantize_out(1, n, out_rounded[1, n])
-        store_codes(1)
+            if n == 1:
+                store_codes(1, slice(0, 2 * BANK))
+        store_codes(1, slice(2 * BANK, M))
         for q in range(QUADRANTS):
             nc.scalar.dma_start(
                 out=out_2[:, 4 * q : 4 * q + 4, :].rearrange("a r n -> r a n").bitcast(I32),

@@ -20,8 +20,13 @@ PACK = 4
 PASS = P * PACK
 BANK = 512
 HALVES = T // PASS
+C_PASSES = L // PASS
 CHUNKS = M // BANK
 QUADRANTS = 4
+PSUM_BANKS = 8
+ROUNDED_TILES = 8
+GPSIMD_CHUNKS = 2
+PC_BANKS_ON_VECTOR = 2
 
 
 def tile_mix_bilin_tm_pl_mul_kernel(tc, x, wx, c, wc, w_words, w_scales, g, out_0, out_1, out_2):
@@ -29,16 +34,25 @@ def tile_mix_bilin_tm_pl_mul_kernel(tc, x, wx, c, wc, w_words, w_scales, g, out_
 
     with ExitStack() as ctx:
         keep = ctx.enter_context(tc.tile_pool(name="keep", bufs=1))
-        stage = ctx.enter_context(tc.tile_pool(name="stage", bufs=8))
-        psum = ctx.enter_context(tc.psum_pool(name="psum", bufs=8))
+        stage = ctx.enter_context(tc.tile_pool(name="stage", bufs=ROUNDED_TILES))
+        psum = ctx.enter_context(tc.psum_pool(name="psum", bufs=PSUM_BANKS))
         ctx.enter_context(tc.manual_schedule())
 
+        def tokens(a):
+            return slice(a * PASS, (a + 1) * PASS)
+
+        def chunk(n):
+            return slice(n * BANK, (n + 1) * BANK)
+
+        def dealt(i):
+            return slice(i * P, (i + 1) * P)
+
+        def row_pair(pair):
+            return slice(2 * pair, 2 * (pair + 1))
+
         def load_pass(name, rows):
-            raw = keep.tile([P, PACK * rows.shape[1]], F32, name=name)
-            nc.sync.dma_start(
-                out=raw[:].rearrange("p (j w) -> p j w", j=PACK),
-                in_=rows.rearrange("(p j) w -> p j w", j=PACK),
-            )
+            raw = keep.tile([P, PACK, BANK], F32, name=name)
+            nc.sync.dma_start(out=raw[:], in_=rows.rearrange("(p j) w -> p j w", j=PACK))
             return raw
 
         def copy_on(engine, out, in_):
@@ -56,12 +70,12 @@ def tile_mix_bilin_tm_pl_mul_kernel(tc, x, wx, c, wc, w_words, w_scales, g, out_
             )
             return rounded
 
-        def round_dealt(engine, raw):
+        def round_dealt(engine, rows):
             rounded = stage.tile([P, PACK * BANK], BF16, tag="rounded", align_bytes=64)
             copy_on(
                 engine,
                 rounded[:].rearrange("p (v e m j) -> p v m j e", v=2, e=2, j=PACK),
-                raw[:].rearrange("p (j m v e) -> p v m j e", v=2, e=2, j=PACK),
+                rows.rearrange("p j (m v e) -> p v m j e", v=2, e=2),
             )
             return rounded
 
@@ -71,45 +85,39 @@ def tile_mix_bilin_tm_pl_mul_kernel(tc, x, wx, c, wc, w_words, w_scales, g, out_
             nc.vector.quantize_mx(out=codes[:].bitcast(fmt), scales=scales[:], in_=rounded[:])
             return codes, scales
 
-        def rows_of(raw):
-            return raw[:].rearrange("p (j w) -> p j w", j=PACK)
+        w_scale_tile = keep.tile([P, M], U8, align_bytes=64)
+        nc.vector.memset(w_scale_tile[:].bitcast(I32), 0)
 
-        def tokens(a):
-            return slice(a * PASS, (a + 1) * PASS)
-
-        w_plane = keep.tile([P, M], U8, align_bytes=64)
-        nc.vector.memset(w_plane[:].bitcast(I32), 0)
-
-        wc_raw, c_raw, x_raw = {}, {}, {}
-        for s in range(2):
-            wc_raw[s] = load_pass("wc_raw%d" % s, wc[s * PASS : (s + 1) * PASS, :])
+        wc_raw = keep.tile([P, C_PASSES, PACK * R], F32)
+        nc.sync.dma_start(out=wc_raw[:], in_=wc.rearrange("(s p j) r -> p s (j r)", p=P, j=PACK))
+        c_raw, x_raw = {}, {}
+        for s in range(C_PASSES):
             c_raw[0, s] = load_pass("c_raw0%d" % s, c[s * PASS : (s + 1) * PASS, tokens(0)])
         for q in range(QUADRANTS):
             nc.scalar.dma_start(
-                out=w_plane[32 * q : 32 * q + 4, :].bitcast(I32),
+                out=w_scale_tile[32 * q : 32 * q + 4, :].bitcast(I32),
                 in_=w_scales[0, 4 * q : 4 * q + 4, :].bitcast(I32),
             )
         wx_raw = load_pass("wx_raw", wx)
         x_raw[0] = load_pass("x_raw0", x[:, tokens(0)])
         w_codes = keep.tile([P, 2 * M], U8, align_bytes=64)
         nc.sync.dma_start(out=w_codes[:].bitcast(I32), in_=w_words[0].bitcast(I32))
-        for s in range(2):
+        for s in range(C_PASSES):
             c_raw[1, s] = load_pass("c_raw1%d" % s, c[s * PASS : (s + 1) * PASS, tokens(1)])
         x_raw[1] = load_pass("x_raw1", x[:, tokens(1)])
+
         gated = {}
         for a in range(HALVES):
             gated[a] = keep.tile([P, PACK, M], F32, name="gated%d" % a)
             g_rows = g[tokens(a), :].rearrange("(p i) n -> p i n", i=PACK)
             for pair in range(2):
-                pair_rows = slice(2 * pair, 2 * (pair + 1))
-                nc.sync.dma_start(out=gated[a][:, pair_rows, :], in_=g_rows[:, pair_rows, :])
+                nc.sync.dma_start(out=gated[a][:, row_pair(pair), :], in_=g_rows[:, row_pair(pair), :])
 
         def c_pass(bank, j, wc_pass, c_pass_q, first):
-            cols = slice(j * P, (j + 1) * P)
             nc.tensor.matmul_mx(
                 out=bank[:],
-                lhsT=wc_pass[0][:, cols].bitcast(E4M3),
-                lhsT_scale=wc_pass[1][:, cols],
+                lhsT=wc_pass[0][:, dealt(j)].bitcast(E4M3),
+                lhsT_scale=wc_pass[1][:, dealt(j)],
                 rhs=c_pass_q[0][:].bitcast(E5M2),
                 rhs_scale=c_pass_q[1][:],
                 start=first,
@@ -124,13 +132,14 @@ def tile_mix_bilin_tm_pl_mul_kernel(tc, x, wx, c, wc, w_words, w_scales, g, out_
                 banks.append(bank)
             return banks
 
-        def close_pc(a, banks, wc_pass, c_pass_q):
+        def close_pc(a, banks, wc_pass, c_pass_q, on_vector):
             pc = keep.tile([P, PACK * BANK], F32, name="pc%d" % a)
             for j in range(PACK):
                 c_pass(banks[j], j, wc_pass, c_pass_q, False)
-                nc.scalar.copy(
-                    out=pc[:, j * BANK : (j + 1) * BANK].rearrange("p (i m) -> p i m", i=PACK),
-                    in_=banks[j][:].rearrange("p (m i) -> p i m", i=PACK),
+                copy_on(
+                    "vector" if j < on_vector else "scalar",
+                    pc[:, chunk(j)].rearrange("p (i m) -> p i m", i=PACK),
+                    banks[j][:].rearrange("p (m i) -> p i m", i=PACK),
                 )
             return pc
 
@@ -139,20 +148,18 @@ def tile_mix_bilin_tm_pl_mul_kernel(tc, x, wx, c, wc, w_words, w_scales, g, out_
             pc_view = pc[:].rearrange("p (j i c u) -> p i c j u", j=PACK, i=PACK, u=2)
             for i in range(PACK):
                 bank = psum.tile([P, BANK], F32, tag="bank")
-                t_cols = slice(i * P, (i + 1) * P)
                 for j in range(PACK):
-                    cols = slice(j * P, (j + 1) * P)
                     nc.tensor.matmul_mx(
-                        out=bank[:, cols],
-                        lhsT=wx_q[0][:, cols].bitcast(E4M3),
-                        lhsT_scale=wx_q[1][:, cols],
-                        rhs=x_q[0][:, t_cols].bitcast(E4M3),
-                        rhs_scale=x_q[1][:, t_cols],
+                        out=bank[:, dealt(j)],
+                        lhsT=wx_q[0][:, dealt(j)].bitcast(E4M3),
+                        lhsT_scale=wx_q[1][:, dealt(j)],
+                        rhs=x_q[0][:, dealt(i)].bitcast(E4M3),
+                        rhs_scale=x_q[1][:, dealt(i)],
                         start=True,
                         stop=True,
                     )
                 nc.vector.tensor_tensor(
-                    out=rounded[:, i * BANK : (i + 1) * BANK].rearrange("p (c u j) -> p c j u", u=2, j=PACK),
+                    out=rounded[:, chunk(i)].rearrange("p (c u j) -> p c j u", u=2, j=PACK),
                     in0=bank[:].rearrange("p (j c u) -> p c j u", j=PACK, u=2),
                     in1=pc_view[:, i],
                     op=MULT,
@@ -161,13 +168,12 @@ def tile_mix_bilin_tm_pl_mul_kernel(tc, x, wx, c, wc, w_words, w_scales, g, out_
 
         def project_h(h_q, i, n):
             bank = psum.tile([P, BANK], F32, tag="bank")
-            cols = slice(i * P, (i + 1) * P)
             nc.tensor.matmul_mx(
                 out=bank[:],
-                lhsT=h_q[0][:, cols].bitcast(E4M3),
-                lhsT_scale=h_q[1][:, cols],
+                lhsT=h_q[0][:, dealt(i)].bitcast(E4M3),
+                lhsT_scale=h_q[1][:, dealt(i)],
                 rhs=w_codes[:, 2 * n * BANK : 2 * (n + 1) * BANK].bitcast(E2M1),
-                rhs_scale=w_plane[:, n * BANK : (n + 1) * BANK],
+                rhs_scale=w_scale_tile[:, chunk(n)],
                 start=True,
                 stop=True,
             )
@@ -175,14 +181,14 @@ def tile_mix_bilin_tm_pl_mul_kernel(tc, x, wx, c, wc, w_words, w_scales, g, out_
 
         def gate(a, h_q, i, n):
             bank = project_h(h_q, i, n)
-            part = gated[a][:, i, n * BANK : (n + 1) * BANK]
+            part = gated[a][:, i, chunk(n)]
             nc.vector.tensor_tensor(out=part, in0=bank[:], in1=part, op=MULT)
 
         def gate_on_gpsimd(a, h_q, i, n):
             bank = project_h(h_q, i, n)
-            y_part = stage.tile([P, BANK], F32, tag="y_part", bufs=4)
+            y_part = stage.tile([P, BANK], F32, tag="y_part", bufs=2 * GPSIMD_CHUNKS)
             nc.scalar.copy(out=y_part[:], in_=bank[:])
-            part = gated[a][:, i, n * BANK : (n + 1) * BANK]
+            part = gated[a][:, i, chunk(n)]
             nc.gpsimd.tensor_tensor(out=part, in0=y_part[:], in1=part, op=MULT)
 
         out_codes = {}
@@ -195,21 +201,20 @@ def tile_mix_bilin_tm_pl_mul_kernel(tc, x, wx, c, wc, w_words, w_scales, g, out_
             copy_on(
                 engine,
                 rounded[:].rearrange("p (n i) -> p n i", i=PACK),
-                gated[a][:, :, n * BANK : (n + 1) * BANK].rearrange("p i n -> p n i"),
+                gated[a][:, :, chunk(n)].rearrange("p i n -> p n i"),
             )
             return rounded
 
         def quantize_out(a, n, rounded):
             nc.vector.quantize_mx(
-                out=out_codes[a][:, n * BANK : (n + 1) * BANK].bitcast(E4M3),
-                scales=out_scales[:, a * M + n * BANK : a * M + (n + 1) * BANK],
+                out=out_codes[a][:, chunk(n)].bitcast(E4M3),
+                scales=out_scales[:, chunk(a * CHUNKS + n)],
                 in_=rounded[:],
             )
 
         def store_pair(a, pair):
-            pair_rows = slice(2 * pair, 2 * (pair + 1))
             out_rows = out_0[tokens(a), :].rearrange("(p i) n -> p i n", i=PACK)
-            nc.sync.dma_start(out=out_rows[:, pair_rows, :], in_=gated[a][:, pair_rows, :])
+            nc.sync.dma_start(out=out_rows[:, row_pair(pair), :], in_=gated[a][:, row_pair(pair), :])
 
         def store_codes(a, cols):
             nc.sync.dma_start(
@@ -218,60 +223,64 @@ def tile_mix_bilin_tm_pl_mul_kernel(tc, x, wx, c, wc, w_words, w_scales, g, out_
             )
 
         wc_q = {}
-        for s in range(2):
-            wc_rounded = round_dealt("scalar", wc_raw[s])
-            c_rounded = round_plain("vector", rows_of(c_raw[0, s]))
+        for s in range(C_PASSES):
+            wc_rounded = round_dealt("scalar", wc_raw[:, s, :].rearrange("p (j r) -> p j r", j=PACK))
+            c_rounded = round_plain("vector", c_raw[0, s][:])
             wc_q[s] = quantize("wc%d" % s, wc_rounded, E4M3)
             c_q = quantize("c0%d" % s, c_rounded, E5M2)
             if s == 0:
                 pc_banks = open_pc(wc_q[0], c_q)
-        pc = close_pc(0, pc_banks, wc_q[1], c_q)
-        wx_q = quantize("wx", round_dealt("vector", wx_raw), E4M3)
-        x_q = quantize("x0", round_dealt("vector", x_raw[0]), E4M3)
-        c_rounded = round_plain("scalar", rows_of(c_raw[1, 0]))
-        h_q = quantize("h0", project_x_and_pool(wx_q, x_q, pc), E4M3)
+        wx_rounded = round_dealt("scalar", wx_raw[:])
+        pc = close_pc(0, pc_banks, wc_q[1], c_q, 0)
+        x_rounded = round_dealt("vector", x_raw[0][:])
+        wx_q = quantize("wx", wx_rounded, E4M3)
+        x_q = quantize("x0", x_rounded, E4M3)
+        h_rounded = project_x_and_pool(wx_q, x_q, pc)
+
+        late_c = [round_plain("scalar", c_raw[1, s][:]) for s in range(C_PASSES)]
+        pc_banks = open_pc(wc_q[0], quantize("c10", late_c[0], E5M2))
+        h_q = {0: quantize("h0", h_rounded, E4M3)}
+        for n in range(GPSIMD_CHUNKS):
+            for i in range(2):
+                gate_on_gpsimd(0, h_q[0], i, n)
+        x_rounded = round_dealt("vector", x_raw[1][:])
+        c_q = quantize("c11", late_c[1], E5M2)
+        x_q = quantize("x1", x_rounded, E4M3)
+        pc = close_pc(1, pc_banks, wc_q[1], c_q, PC_BANKS_ON_VECTOR)
+        for n in range(GPSIMD_CHUNKS, CHUNKS):
+            for i in range(2):
+                gate(0, h_q[0], i, n)
+        store_pair(0, 0)
+        h_rounded = project_x_and_pool(wx_q, x_q, pc)
 
         out_rounded = {}
-        for n in range(CHUNKS - 1):
-            for i in range(2):
-                gate_on_gpsimd(0, h_q, i, n)
-        c_q = quantize("c10", c_rounded, E5M2)
-        pc_banks = open_pc(wc_q[0], c_q)
-        c_rounded = round_plain("vector", rows_of(c_raw[1, 1]))
-        x_rounded = round_dealt("vector", x_raw[1])
-        c_q = quantize("c11", c_rounded, E5M2)
-        x_q = quantize("x1", x_rounded, E4M3)
-        pc = close_pc(1, pc_banks, wc_q[1], c_q)
-        h_rounded = project_x_and_pool(wx_q, x_q, pc)
-        for i in range(2):
-            gate(0, h_q, i, CHUNKS - 1)
-        store_pair(0, 0)
         for n in range(CHUNKS):
             for i in range(2, PACK):
-                gate(0, h_q, i, n)
+                gate(0, h_q[0], i, n)
             out_rounded[0, n] = round_out("scalar", 0, n)
-            if n == 1:
-                h_next = quantize("h1", h_rounded, E4M3)
+            if n == CHUNKS - 2:
+                h_q[1] = quantize("h1", h_rounded, E4M3)
         store_pair(0, 1)
 
-        h_q = h_next
         for i in range(2):
             for n in range(CHUNKS):
-                gate(1, h_q, i, n)
+                gate(1, h_q[1], i, n)
             quantize_out(0, i, out_rounded[0, i])
-        quantize_out(0, 2, out_rounded[0, 2])
-        store_codes(0, slice(0, M))
         store_pair(1, 0)
         for n in (0, 2, 1):
             for i in range(2, PACK):
-                gate(1, h_q, i, n)
+                gate(1, h_q[1], i, n)
             out_rounded[1, n] = round_out("vector" if n == 1 else "scalar", 1, n)
+            if n == 0:
+                quantize_out(0, 2, out_rounded[0, 2])
+                store_codes(0, slice(0, M))
         store_pair(1, 1)
-        for n in range(CHUNKS):
+        for n in range(CHUNKS - 1):
             quantize_out(1, n, out_rounded[1, n])
-            if n == 1:
-                store_codes(1, slice(0, 2 * BANK))
-        store_codes(1, slice(2 * BANK, M))
+        store_codes(1, slice(0, M - BANK))
+        quantize_out(1, CHUNKS - 1, out_rounded[1, CHUNKS - 1])
+        store_codes(1, chunk(CHUNKS - 1))
+
         for q in range(QUADRANTS):
             nc.scalar.dma_start(
                 out=out_2[:, 4 * q : 4 * q + 4, :].rearrange("a r n -> r a n").bitcast(I32),

from contextlib import ExitStack

import concourse.mybir as mybir

K, L, R, M, T = 512, 1024, 512, 1536, 1024
FLOPS = 2 * (K * R * T + L * R * T + R * T * M)

F32 = mybir.dt.float32
BF16 = mybir.dt.bfloat16
I32 = mybir.dt.int32
U32 = mybir.dt.uint32
U8 = mybir.dt.uint8
E4M3 = mybir.dt.float8_e4m3fn_x4
E5M2 = mybir.dt.float8_e5m2_x4
E2M1 = mybir.dt.float4_e2m1fn_x4
MULT = mybir.AluOpType.mult

P = 128
PACK = 4
PASS = P * PACK
BANK = 512
HALVES = T // PASS
C_PASSES = L // PASS
CHUNKS = M // BANK
QUADRANTS = 4
PSUM_BANKS = 8
ROUNDED_TILES = 8
GPSIMD_CHUNKS = 2
PC_BANKS_ON_VECTOR = 2


def tile_mix_bilin_tm_pl_mul_kernel(tc, x, wx, c, wc, w_words, w_scales, g, out_0, out_1, out_2):
    nc = tc.nc

    with ExitStack() as ctx:
        keep = ctx.enter_context(tc.tile_pool(name="keep", bufs=1))
        stage = ctx.enter_context(tc.tile_pool(name="stage", bufs=ROUNDED_TILES))
        psum = ctx.enter_context(tc.psum_pool(name="psum", bufs=PSUM_BANKS))
        ctx.enter_context(tc.manual_schedule())

        def tokens(a):
            return slice(a * PASS, (a + 1) * PASS)

        def chunk(n):
            return slice(n * BANK, (n + 1) * BANK)

        def dealt(i):
            return slice(i * P, (i + 1) * P)

        def row_pair(pair):
            return slice(2 * pair, 2 * (pair + 1))

        def load_pass(name, rows):
            raw = keep.tile([P, PACK, BANK], F32, name=name)
            nc.sync.dma_start(out=raw[:], in_=rows.rearrange("(p j) w -> p j w", j=PACK))
            return raw

        def copy_on(engine, out, in_):
            if engine == "scalar":
                nc.scalar.copy(out=out, in_=in_)
            else:
                nc.vector.tensor_copy(out=out, in_=in_)

        def round_plain(engine, rows):
            rounded = stage.tile([P, PACK * BANK], BF16, tag="rounded", align_bytes=64)
            copy_on(
                engine,
                rounded[:].rearrange("p (c u j) -> p c j u", u=4, j=PACK),
                rows.rearrange("p j (c u) -> p c j u", u=4),
            )
            return rounded

        def round_dealt(engine, rows):
            rounded = stage.tile([P, PACK * BANK], BF16, tag="rounded", align_bytes=64)
            copy_on(
                engine,
                rounded[:].rearrange("p (v e m j) -> p v m j e", v=2, e=2, j=PACK),
                rows.rearrange("p j (m v e) -> p v m j e", v=2, e=2),
            )
            return rounded

        def quantize(name, rounded, fmt):
            codes = keep.tile([P, BANK], U32, name=name + "_codes", align_bytes=64)
            scales = keep.tile([P, BANK], U8, name=name + "_scales", align_bytes=64)
            nc.vector.quantize_mx(out=codes[:].bitcast(fmt), scales=scales[:], in_=rounded[:])
            return codes, scales

        w_scale_tile = keep.tile([P, M], U8, align_bytes=64)
        nc.vector.memset(w_scale_tile[:].bitcast(I32), 0)

        wc_raw = keep.tile([P, C_PASSES, PACK * R], F32)
        nc.sync.dma_start(out=wc_raw[:], in_=wc.rearrange("(s p j) r -> p s (j r)", p=P, j=PACK))
        c_raw, x_raw = {}, {}
        for s in range(C_PASSES):
            c_raw[0, s] = load_pass("c_raw0%d" % s, c[s * PASS : (s + 1) * PASS, tokens(0)])
        for q in range(QUADRANTS):
            nc.scalar.dma_start(
                out=w_scale_tile[32 * q : 32 * q + 4, :].bitcast(I32),
                in_=w_scales[0, 4 * q : 4 * q + 4, :].bitcast(I32),
            )
        wx_raw = load_pass("wx_raw", wx)
        x_raw[0] = load_pass("x_raw0", x[:, tokens(0)])
        w_codes = keep.tile([P, 2 * M], U8, align_bytes=64)
        nc.sync.dma_start(out=w_codes[:].bitcast(I32), in_=w_words[0].bitcast(I32))
        for s in range(C_PASSES):
            c_raw[1, s] = load_pass("c_raw1%d" % s, c[s * PASS : (s + 1) * PASS, tokens(1)])
        x_raw[1] = load_pass("x_raw1", x[:, tokens(1)])

        gated = {}
        for a in range(HALVES):
            gated[a] = keep.tile([P, PACK, M], F32, name="gated%d" % a)
            g_rows = g[tokens(a), :].rearrange("(p i) n -> p i n", i=PACK)
            for pair in range(2):
                nc.sync.dma_start(out=gated[a][:, row_pair(pair), :], in_=g_rows[:, row_pair(pair), :])

        def c_pass(bank, j, wc_pass, c_pass_q, first):
            nc.tensor.matmul_mx(
                out=bank[:],
                lhsT=wc_pass[0][:, dealt(j)].bitcast(E4M3),
                lhsT_scale=wc_pass[1][:, dealt(j)],
                rhs=c_pass_q[0][:].bitcast(E5M2),
                rhs_scale=c_pass_q[1][:],
                start=first,
                stop=not first,
            )

        def open_pc(wc_pass, c_pass_q):
            banks = []
            for j in range(PACK):
                bank = psum.tile([P, BANK], F32, tag="bank")
                c_pass(bank, j, wc_pass, c_pass_q, True)
                banks.append(bank)
            return banks

        def close_pc(a, banks, wc_pass, c_pass_q, on_vector):
            pc = keep.tile([P, PACK * BANK], F32, name="pc%d" % a)
            for j in range(PACK):
                c_pass(banks[j], j, wc_pass, c_pass_q, False)
                copy_on(
                    "vector" if j < on_vector else "scalar",
                    pc[:, chunk(j)].rearrange("p (i m) -> p i m", i=PACK),
                    banks[j][:].rearrange("p (m i) -> p i m", i=PACK),
                )
            return pc

        def project_x_and_pool(wx_q, x_q, pc):
            rounded = stage.tile([P, PACK * BANK], BF16, tag="rounded", align_bytes=64)
            pc_view = pc[:].rearrange("p (j i c u) -> p i c j u", j=PACK, i=PACK, u=2)
            for i in range(PACK):
                bank = psum.tile([P, BANK], F32, tag="bank")
                for j in range(PACK):
                    nc.tensor.matmul_mx(
                        out=bank[:, dealt(j)],
                        lhsT=wx_q[0][:, dealt(j)].bitcast(E4M3),
                        lhsT_scale=wx_q[1][:, dealt(j)],
                        rhs=x_q[0][:, dealt(i)].bitcast(E4M3),
                        rhs_scale=x_q[1][:, dealt(i)],
                        start=True,
                        stop=True,
                    )
                nc.vector.tensor_tensor(
                    out=rounded[:, chunk(i)].rearrange("p (c u j) -> p c j u", u=2, j=PACK),
                    in0=bank[:].rearrange("p (j c u) -> p c j u", j=PACK, u=2),
                    in1=pc_view[:, i],
                    op=MULT,
                )
            return rounded

        def project_h(h_q, i, n):
            bank = psum.tile([P, BANK], F32, tag="bank")
            nc.tensor.matmul_mx(
                out=bank[:],
                lhsT=h_q[0][:, dealt(i)].bitcast(E4M3),
                lhsT_scale=h_q[1][:, dealt(i)],
                rhs=w_codes[:, 2 * n * BANK : 2 * (n + 1) * BANK].bitcast(E2M1),
                rhs_scale=w_scale_tile[:, chunk(n)],
                start=True,
                stop=True,
            )
            return bank

        def gate(a, h_q, i, n):
            bank = project_h(h_q, i, n)
            part = gated[a][:, i, chunk(n)]
            nc.vector.tensor_tensor(out=part, in0=bank[:], in1=part, op=MULT)

        def gate_on_gpsimd(a, h_q, i, n):
            bank = project_h(h_q, i, n)
            y_part = stage.tile([P, BANK], F32, tag="y_part", bufs=2 * GPSIMD_CHUNKS)
            nc.scalar.copy(out=y_part[:], in_=bank[:])
            part = gated[a][:, i, chunk(n)]
            nc.gpsimd.tensor_tensor(out=part, in0=y_part[:], in1=part, op=MULT)

        out_codes = {}
        for a in range(HALVES):
            out_codes[a] = keep.tile([P, M], U32, name="out_codes%d" % a, align_bytes=64)
        out_scales = keep.tile([P, HALVES * M], U8, align_bytes=64)

        def round_out(engine, a, n):
            rounded = stage.tile([P, PACK * BANK], BF16, tag="rounded", align_bytes=64)
            copy_on(
                engine,
                rounded[:].rearrange("p (n i) -> p n i", i=PACK),
                gated[a][:, :, chunk(n)].rearrange("p i n -> p n i"),
            )
            return rounded

        def quantize_out(a, n, rounded):
            nc.vector.quantize_mx(
                out=out_codes[a][:, chunk(n)].bitcast(E4M3),
                scales=out_scales[:, chunk(a * CHUNKS + n)],
                in_=rounded[:],
            )

        def store_pair(a, pair):
            out_rows = out_0[tokens(a), :].rearrange("(p i) n -> p i n", i=PACK)
            nc.sync.dma_start(out=out_rows[:, row_pair(pair), :], in_=gated[a][:, row_pair(pair), :])

        def store_codes(a, cols):
            nc.sync.dma_start(
                out=out_1[a].rearrange("p n i -> p (n i)").bitcast(I32)[:, cols],
                in_=out_codes[a][:, cols].bitcast(I32),
            )

        wc_q = {}
        for s in range(C_PASSES):
            wc_rounded = round_dealt("scalar", wc_raw[:, s, :].rearrange("p (j r) -> p j r", j=PACK))
            c_rounded = round_plain("vector", c_raw[0, s][:])
            wc_q[s] = quantize("wc%d" % s, wc_rounded, E4M3)
            c_q = quantize("c0%d" % s, c_rounded, E5M2)
            if s == 0:
                pc_banks = open_pc(wc_q[0], c_q)
        wx_rounded = round_dealt("scalar", wx_raw[:])
        pc = close_pc(0, pc_banks, wc_q[1], c_q, 0)
        x_rounded = round_dealt("vector", x_raw[0][:])
        wx_q = quantize("wx", wx_rounded, E4M3)
        x_q = quantize("x0", x_rounded, E4M3)
        h_rounded = project_x_and_pool(wx_q, x_q, pc)

        late_c = [round_plain("scalar", c_raw[1, s][:]) for s in range(C_PASSES)]
        pc_banks = open_pc(wc_q[0], quantize("c10", late_c[0], E5M2))
        h_q = {0: quantize("h0", h_rounded, E4M3)}
        for n in range(GPSIMD_CHUNKS):
            for i in range(2):
                gate_on_gpsimd(0, h_q[0], i, n)
        x_rounded = round_dealt("vector", x_raw[1][:])
        c_q = quantize("c11", late_c[1], E5M2)
        x_q = quantize("x1", x_rounded, E4M3)
        pc = close_pc(1, pc_banks, wc_q[1], c_q, PC_BANKS_ON_VECTOR)
        for n in range(GPSIMD_CHUNKS, CHUNKS):
            for i in range(2):
                gate(0, h_q[0], i, n)
        store_pair(0, 0)
        h_rounded = project_x_and_pool(wx_q, x_q, pc)

        out_rounded = {}
        for n in range(CHUNKS):
            for i in range(2, PACK):
                gate(0, h_q[0], i, n)
            out_rounded[0, n] = round_out("scalar", 0, n)
            if n == CHUNKS - 2:
                h_q[1] = quantize("h1", h_rounded, E4M3)
        store_pair(0, 1)

        for i in range(2):
            for n in range(CHUNKS):
                gate(1, h_q[1], i, n)
            quantize_out(0, i, out_rounded[0, i])
        store_pair(1, 0)
        for n in (0, 2, 1):
            for i in range(2, PACK):
                gate(1, h_q[1], i, n)
            out_rounded[1, n] = round_out("vector" if n == 1 else "scalar", 1, n)
            if n == 0:
                quantize_out(0, 2, out_rounded[0, 2])
                store_codes(0, slice(0, M))
        store_pair(1, 1)
        for n in range(CHUNKS - 1):
            quantize_out(1, n, out_rounded[1, n])
        store_codes(1, slice(0, M - BANK))
        quantize_out(1, CHUNKS - 1, out_rounded[1, CHUNKS - 1])
        store_codes(1, chunk(CHUNKS - 1))

        for q in range(QUADRANTS):
            nc.scalar.dma_start(
                out=out_2[:, 4 * q : 4 * q + 4, :].rearrange("a r n -> r a n").bitcast(I32),
                in_=out_scales[32 * q : 32 * q + 4, :].bitcast(I32).rearrange("r (a n) -> r a n", a=HALVES),
            )
